import numpy as np
import ml_dtypes


def mxq(x, axis, fmt="e4m3"):
    dtype, down = {"e4m3": (ml_dtypes.float8_e4m3fn, 7), "e5m2": (ml_dtypes.float8_e5m2, 14)}[fmt]
    v = np.moveaxis(np.asarray(x, np.float32).astype(ml_dtypes.bfloat16).astype(np.float64), axis, -1)
    blocks = v.reshape(v.shape[:-1] + (-1, 32))
    amax = np.abs(blocks).max(-1, keepdims=True)
    byte = np.maximum(np.where(amax > 0, np.frexp(amax)[1] - 1 + 127, 0) - down, 1)
    scale = np.exp2(byte - 127.0)
    codes = (blocks / scale).astype(np.float32).astype(dtype).astype(np.float64)
    return np.moveaxis((codes * scale).reshape(v.shape), -1, axis)


WIDE = False


def mx_kscale(k):
    if not WIDE:
        return np.ones(k)
    levels = np.array([10, -10, 5, -5, 0])
    if k % 512:
        return np.exp2(np.random.permutation(np.resize(levels, k // 32))).repeat(32)
    a = np.empty((k // 512, 16))
    for p in range(k // 512):
        a[p, :8] = np.random.permutation(np.resize(levels, 8))
        for g in range(8):
            far = levels[np.abs(levels - a[p, g]) >= 10]
            a[p, g + 8] = far[np.random.randint(len(far))]
    return np.exp2(a.ravel()).repeat(32)


def f64(x):
    return np.asarray(x).astype(np.float64)


def striped(idx):
    return np.tile(idx.reshape(-1, 16).T, (8, 1)).astype(np.uint16)


def unstriped(offs):
    return offs[:16].T.reshape(-1).astype(np.int64)


def striped8(idx):
    return np.concatenate([x.reshape(-1, 16).T for x in idx]).astype(np.uint16)


def runs(offs, k):
    lists = np.stack([offs[16 * r : 16 * r + 16].T.reshape(-1) for r in range(8)]).astype(np.int64)
    return lists[np.arange(k) % 512 // 64]


def pack_weight(w):
    k, n = w.shape
    w = f64(np.asarray(w, np.float32).astype(ml_dtypes.bfloat16)).reshape(k // 32, 32, n)
    amax = np.abs(w).max(1)
    byte = np.clip(np.where(amax > 0, np.frexp(amax)[1] - 1 + 127 - 7, 1), 1, 254)
    scaled = (w * np.exp2(127.0 - byte)[:, None, :]).reshape(k, n).astype(np.float32)
    words = np.ascontiguousarray(scaled.reshape(k // 512, 128, 4, n).transpose(0, 1, 3, 2)).astype(ml_dtypes.float8_e4m3fn).view(np.uint8)
    return words, np.ascontiguousarray(byte.astype(np.uint8).reshape(k // 512, 16, n))


def unpack_weight(words, scales):
    g, p, n, _ = words.shape
    vals = np.ascontiguousarray(words).view(ml_dtypes.float8_e4m3fn).astype(np.float64) * np.repeat(np.exp2(scales.astype(np.float64) - 127.0), 8, axis=1)[..., None]
    return vals.transpose(0, 1, 3, 2).reshape(g * 512, n)

def planes(y):
    n, m = y.shape
    v = y.astype(np.float32).astype(ml_dtypes.bfloat16).astype(np.float64).reshape(n // 32, 32, m)
    top = np.abs(v).max(1)
    byte = np.clip(np.where(top > 0, np.frexp(top)[1] - 1 + 127 - 7, 1), 1, 254)
    codes = (v * np.exp2(127.0 - byte)[:, None, :]).reshape(n, m).astype(np.float32).astype(ml_dtypes.float8_e4m3fn).view(np.uint8)
    words = codes.reshape(n // 512, 128, 4, m).transpose(0, 1, 3, 2)
    return np.ascontiguousarray(words), np.ascontiguousarray(byte.astype(np.uint8).reshape(n // 512, 16, m))


K, T, S, H, C = 512, 2048, 256, 512, 512


def setup_inputs():
    n = np.random.standard_normal
    s = mx_kscale(K)[:, None]
    packed_xT = pack_weight(n((K, T)) * s)
    packed_w1 = pack_weight(n((K, H)) / np.sqrt(K) / s)
    packed_w2 = pack_weight(n((K, H)) / np.sqrt(K) / s)
    return {
        "x_words": packed_xT[0],
        "x_scales": packed_xT[1],
        "w1_words": packed_w1[0],
        "w1_scales": packed_w1[1],
        "w2_words": packed_w2[0],
        "w2_scales": packed_w2[1],
        "gs": (np.random.uniform(0.5, 1.5, (K, 1)) / s).astype(np.float32),
        "offs": striped(np.random.permutation(T)[:S]),
        "two": striped(np.random.permutation(T)[:S]),
        "n1": striped(np.random.permutation(S)),
        "n2": striped(np.random.permutation(S)),
        "n3": striped(np.random.permutation(S)),
        "cand": striped(np.random.permutation(T)[:C]),
        "n4": striped8(np.stack([np.random.permutation(S) for _ in range(8)])),
        "n5": striped8(np.stack([np.random.permutation(S) for _ in range(8)])),
    }


def reference(x_words, x_scales, w1_words, w1_scales, w2_words, w2_scales, gs, offs, two, n1, n2, n3, cand, n4, n5):
    x_cand = unpack_weight(x_words, x_scales)[:, unstriped(cand)]
    xq = unpack_weight(x_words, x_scales)[:, unstriped(offs)]
    y = unpack_weight(w1_words, w1_scales).T @ xq
    x_two = unpack_weight(x_words, x_scales)[:, unstriped(two)]
    d = unpack_weight(w2_words, w2_scales).T @ x_two
    z = f64(gs) * (np.maximum(np.minimum(y - (0.5 * y[:, unstriped(n1)]), d[:, unstriped(n2)]), d[:, unstriped(n3)]))
    s = 0.0625 * ((x_cand.T @ mxq(z, 0, "e4m3")))
    out_0 = (s - (s[np.arange(C)[:, None], runs(n4, C)])) / (np.abs(s[np.arange(C)[:, None], runs(n5, C)] - s) + 0.5)
    return (out_0,) + planes(out_0)

@@ -1,0 +1,211 @@
+from contextlib import ExitStack
+
+import concourse.mybir as mybir
+
+K, T, S, H, C = 512, 2048, 256, 512, 512
+FLOPS = 2 * K * H * S * 2 + 2 * K * C * S
+
+F32 = mybir.dt.float32
+BF16 = mybir.dt.bfloat16
+I32 = mybir.dt.int32
+U32 = mybir.dt.uint32
+U16 = mybir.dt.uint16
+U8 = mybir.dt.uint8
+FP8X4 = mybir.dt.float8_e4m3fn_x4
+ALU = mybir.AluOpType
+ACT = mybir.ActivationFunctionType
+
+P = 128
+PACK = 4
+HALF = S // 2
+QUADS = 4
+
+
+def tile_picked_twcclampbfrac_none_po_kernel(
+    tc, x_words, x_scales, w1_words, w1_scales, w2_words, w2_scales, gs, offs, two, n1, n2, n3, cand, n4, n5, out_0, out_1, out_2
+):
+    nc = tc.nc
+    with ExitStack() as ctx:
+        sb = ctx.enter_context(tc.tile_pool(name="sb", bufs=1))
+        psum = ctx.enter_context(tc.psum_pool(name="psum", bufs=1))
+
+        def tile(name, shape, dtype):
+            return sb.tile(shape, dtype, name=name, align_bytes=64)
+
+        def load_list(name, src):
+            dst = tile(name, [P, src.shape[1]], U16)
+            nc.sync.dma_start(dst[:], src)
+            return dst
+
+        def load_words(name, src):
+            dst = tile(name, [P, src.shape[2]], U32)
+            nc.sync.dma_start(dst[:].bitcast(I32), src[0].rearrange("p n t -> p (n t)").bitcast(I32))
+            return dst
+
+        def zeroed_plane(name, width):
+            dst = tile(name, [P, width], U8)
+            nc.vector.memset(dst[:].bitcast(I32), 0)
+            return dst
+
+        def load_scale_rows(queue, dst, src, q, first):
+            queue.dma_start(dst[32 * q + first : 32 * q + first + 4, :].bitcast(I32), src[0, 4 * q : 4 * q + 4, :].bitcast(I32))
+
+        def deal(name, src, dtype, view):
+            dst = tile(name, [P, PACK * P], dtype)
+            nc.vector.tensor_copy(
+                dst[:].bitcast(view).rearrange("p (t m) -> p m t", t=PACK),
+                src[:].bitcast(view).rearrange("p (m t) -> p m t", t=PACK),
+            )
+            return dst
+
+        def pick(name, table, offsets, dtype):
+            dst = tile(name, [P, 16 * offsets.shape[1]], dtype)
+            nc.vector.tensor_copy(dst[:], table[:].indirect(offsets[:]))
+            return dst
+
+        def fetch(dst, window, offsets, h):
+            nc.scalar.activation(dst, window[:].indirect(offsets[:, 8 * h : 8 * h + 8]), ACT.Copy)
+
+        def cols(h):
+            return slice(HALF * h, HALF * (h + 1))
+
+        W2_ROW, W1_ROW = 4, 8
+
+        w2s_raw = zeroed_plane("w2s_raw", H)
+        xs = zeroed_plane("xs", T)
+        w1s_raw = zeroed_plane("w1s_raw", H)
+        half_col = tile("half_col", [P, 1], F32)
+        nc.vector.memset(half_col[:], 0.5)
+
+        w2w_raw = load_words("w2w_raw", w2_words)
+        two_l = load_list("two_l", two)
+        for q in range(QUADS):
+            load_scale_rows(nc.sync, w2s_raw, w2_scales, q, W2_ROW)
+        xw = load_words("xw", x_words)
+        offs_l = load_list("offs_l", offs)
+        for q in range(QUADS):
+            load_scale_rows(nc.sync, xs, x_scales, q, 0)
+        n2_l = load_list("n2_l", n2)
+        w1w_raw = load_words("w1w_raw", w1_words)
+        cand_l = load_list("cand_l", cand)
+        for q in range(QUADS):
+            load_scale_rows(nc.sync, w1s_raw, w1_scales, q, W1_ROW)
+        n1_l = load_list("n1_l", n1)
+        n3_l = load_list("n3_l", n3)
+        gain = tile("gain", [P, PACK], F32)
+        nc.sync.dma_start(gain[:], gs.rearrange("(p t) o -> p (t o)", t=PACK))
+        n5_l = load_list("n5_l", n5)
+        n4_l = load_list("n4_l", n4)
+
+        def product(out, lw, ls, first, t, rw, rs):
+            m = slice(P * t, P * (t + 1))
+            nc.tensor.matmul_mx(out, lhsT=lw[:, m].bitcast(FP8X4), lhsT_scale=ls[first:P, m], rhs=rw.bitcast(FP8X4), rhs_scale=rs, start=True, stop=True)
+
+        w2w = deal("w2w", w2w_raw, U32, I32)
+        w2s = deal("w2s", w2s_raw, U8, U8)
+        two_w = pick("two_w", xw, two_l, U32)
+        two_s = pick("two_s", xs, two_l, U8)
+        d = []
+        for t in range(PACK):
+            bank = psum.tile([P, S], F32, name=f"d_ps{t}", tag=f"bank{t}")
+            product(bank[:], w2w, w2s, W2_ROW, t, two_w[:], two_s[:])
+            d_t = tile(f"d{t}", [P, S], F32)
+            nc.scalar.activation(d_t[:], bank[:], ACT.Copy)
+            d.append(d_t)
+
+        offs_w = pick("offs_w", xw, offs_l, U32)
+        offs_s = pick("offs_s", xs, offs_l, U8)
+        w1w = deal("w1w", w1w_raw, U32, I32)
+        w1s = deal("w1s", w1s_raw, U8, U8)
+        y_ps = [psum.tile([P, 2, S], F32, name=f"y_ps{u}", tag=f"bank{4 + u}") for u in range(2)]
+        for t in range(PACK):
+            product(y_ps[t // 2][:, t % 2, :], w1w, w1s, W1_ROW, t, offs_w[:], offs_s[:])
+
+        cand_w = deal("cand_w", pick("cand_w_raw", xw, cand_l, U32), U32, I32)
+        cand_s = deal("cand_s", pick("cand_s_raw", xs, cand_l, U8), U8, U8)
+
+        g1 = [tile(f"g1_{h}", [P, PACK, HALF], F32) for h in range(2)]
+        g2 = [tile(f"g2_{h}", [P, PACK, HALF], F32) for h in range(2)]
+        g3 = [tile(f"g3_{h}", [P, PACK, HALF], F32) for h in range(2)]
+        y = [tile(f"y{t}", [P, S], F32) for t in range(PACK)]
+        s = [tile(f"s{t}", [P, S], F32) for t in range(PACK)]
+
+        def blocked_rows(ap):
+            return ap.rearrange("p t (c i) -> p c t i", i=4)
+
+        def blocked_words(ap):
+            return ap.rearrange("p (c i t) -> p c t i", i=4, t=PACK)
+
+        for t in range(PACK):
+            fetch(g2[0][:, t, :], d[t], n2_l, 0)
+        for t in range(PACK):
+            nc.scalar.activation(y[t][:], y_ps[t // 2][:, t % 2, :], ACT.Copy)
+
+        for h in range(2):
+            less = tile(f"less{h}", [P, PACK, HALF], F32)
+            low = tile(f"low{h}", [P, PACK, HALF], F32)
+            top = tile(f"top{h}", [P, PACK, HALF], F32)
+            for t in range(PACK):
+                fetch(g1[h][:, t, :], y[t], n1_l, h)
+                nc.vector.scalar_tensor_tensor(less[:, t, :], g1[h][:, t, :], -0.5, y[t][:, cols(h)], ALU.mult, ALU.add)
+            if h == 1:
+                for t in range(PACK):
+                    fetch(g2[h][:, t, :], d[t], n2_l, h)
+            for u in range(2):
+                tt = slice(2 * u, 2 * u + 2)
+                nc.vector.tensor_tensor(low[:, tt, :], less[:, tt, :], g2[h][:, tt, :], ALU.min)
+            for t in range(PACK):
+                fetch(g3[h][:, t, :], d[t], n3_l, h)
+            for u in range(2):
+                tt = slice(2 * u, 2 * u + 2)
+                nc.vector.tensor_tensor(top[:, tt, :], low[:, tt, :], g3[h][:, tt, :], ALU.max)
+            z = tile(f"z{h}", [P, PACK * HALF], BF16)
+            gain_b = gain[:].unsqueeze(1).unsqueeze(3).to_broadcast([P, HALF // 4, PACK, 4])
+            nc.vector.tensor_tensor(blocked_words(z[:]), blocked_rows(top[:]), gain_b, ALU.mult)
+            zw = tile(f"zw{h}", [P, HALF], U32)
+            zs = tile(f"zs{h}", [P, HALF], U8)
+            nc.vector.quantize_mx(out=zw[:].bitcast(FP8X4), scales=zs[:], in_=z[:])
+            for t in range(PACK):
+                bank = psum.tile([P, HALF], F32, name=f"s_ps{h}_{t}", tag=f"bank{(4 + 4 * h + t) % 8}")
+                product(bank[:], cand_w, cand_s, 0, t, zw[:], zs[:])
+                if h == 1 and t % 2 == 1:
+                    nc.vector.tensor_scalar(s[t][:, cols(h)], bank[:], 0.0625, None, ALU.mult)
+                else:
+                    nc.scalar.activation(s[t][:, cols(h)], bank[:], ACT.Copy, scale=0.0625)
+
+        g4 = [tile(f"g4_{h}", [P, PACK, HALF], F32) for h in range(2)]
+        g5 = [tile(f"g5_{h}", [P, PACK, HALF], F32) for h in range(2)]
+        size = []
+        for h in range(2):
+            diff = tile(f"diff{h}", [P, PACK, HALF], F32)
+            size_h = tile(f"size{h}", [P, PACK * HALF], F32)
+            for t in range(PACK):
+                fetch(g5[h][:, t, :], s[t], n5_l, h)
+                nc.vector.tensor_tensor(diff[:, t, :], g5[h][:, t, :], s[t][:, cols(h)], ALU.subtract)
+            flat = diff[:].rearrange("p t j -> p (t j)")
+            nc.vector.scalar_tensor_tensor(size_h[:], flat, -1.0, flat, ALU.mult, ALU.max)
+            size.append(size_h)
+
+        out_rows = out_0.rearrange("(p t) j -> p t j", t=PACK)
+        for h in range(2):
+            root = tile(f"root{h}", [P, PACK * HALF], F32)
+            inv = tile(f"inv{h}", [P, PACK * HALF], F32)
+            num = tile(f"num{h}", [P, PACK, HALF], F32)
+            res = tile(f"res{h}", [P, PACK, HALF], F32)
+            nc.scalar.activation(root[:], size[h][:], ACT.Abs_reciprocal_sqrt, bias=half_col[:])
+            nc.vector.tensor_tensor(inv[:], root[:], root[:], ALU.mult)
+            for t in range(PACK):
+                fetch(g4[h][:, t, :], s[t], n4_l, h)
+                nc.vector.tensor_tensor(num[:, t, :], s[t][:, cols(h)], g4[h][:, t, :], ALU.subtract)
+            nc.vector.tensor_tensor(res[:].rearrange("p t j -> p (t j)"), num[:].rearrange("p t j -> p (t j)"), inv[:], ALU.mult)
+            nc.sync.dma_start(out_rows[:, :, cols(h)], res[:])
+            rounded = tile(f"rounded{h}", [P, PACK * HALF], BF16)
+            nc.vector.tensor_copy(blocked_words(rounded[:]), blocked_rows(res[:]))
+            ow = tile(f"ow{h}", [P, HALF], U32)
+            osc = tile(f"osc{h}", [P, HALF], U8)
+            nc.vector.quantize_mx(out=ow[:].bitcast(FP8X4), scales=osc[:], in_=rounded[:])
+            words_out = out_1[0].rearrange("p n t -> p (n t)").bitcast(I32)
+            nc.sync.dma_start(words_out[:, cols(h)], ow[:].bitcast(I32))
+            for q in range(QUADS):
+                queue = nc.scalar if q % 2 == 0 else nc.sync
+                queue.dma_start(out_2[0, 4 * q : 4 * q + 4, cols(h)].bitcast(I32), osc[32 * q : 32 * q + 4, :].bitcast(I32))

@@ -29,8 +29,8 @@ def tile_picked_twcclampbfrac_none_po_kernel(
         sb = ctx.enter_context(tc.tile_pool(name="sb", bufs=1))
         psum = ctx.enter_context(tc.psum_pool(name="psum", bufs=1))
 
-        def tile(name, shape, dtype):
-            return sb.tile(shape, dtype, name=name, align_bytes=64)
+        def tile(name, shape, dtype, tag=None):
+            return sb.tile(shape, dtype, name=name, tag=tag or name, align_bytes=64)
 
         def load_list(name, src):
             dst = tile(name, [P, src.shape[1]], U16)
@@ -58,13 +58,21 @@ def tile_picked_twcclampbfrac_none_po_kernel(
             )
             return dst
 
-        def pick(name, table, offsets, dtype):
-            dst = tile(name, [P, 16 * offsets.shape[1]], dtype)
+        def pick(name, table, offsets, dtype, tag=None):
+            dst = tile(name, [P, 16 * offsets.shape[1]], dtype, tag=tag)
             nc.vector.tensor_copy(dst[:], table[:].indirect(offsets[:]))
             return dst
 
-        def fetch(dst, window, offsets, h):
-            nc.scalar.activation(dst, window[:].indirect(offsets[:, 8 * h : 8 * h + 8]), ACT.Copy)
+        def fetch(dst, window, offsets):
+            nc.scalar.activation(dst, window[:].indirect(offsets), ACT.Copy)
+
+        def entries(offsets, h):
+            return offsets[:, 8 * h : 8 * h + 8]
+
+        def window_tile(name, width):
+            dst = tile(name, [P, width], F32)
+            nc.vector.memset(dst[:, S:width], 0.0)
+            return dst
 
         def cols(h):
             return slice(HALF * h, HALF * (h + 1))
@@ -73,23 +81,25 @@ def tile_picked_twcclampbfrac_none_po_kernel(
 
         w2s_raw = zeroed_plane("w2s_raw", H)
         xs = zeroed_plane("xs", T)
-        w1s_raw = zeroed_plane("w1s_raw", H)
+        w1s_raw = tile("w1s_raw", [P, H], U8)
+        nc.gpsimd.memset(w1s_raw[:].bitcast(I32), 0)
+        for q in range(QUADS):
+            load_scale_rows(nc.gpsimd, w1s_raw, w1_scales, q, W1_ROW)
         half_col = tile("half_col", [P, 1], F32)
         nc.vector.memset(half_col[:], 0.5)
-
+        warm = tile("warm", [P, 1], F32)
+        nc.scalar.activation(warm[:], half_col[:], ACT.Abs_reciprocal_sqrt, bias=half_col[:])
         w2w_raw = load_words("w2w_raw", w2_words)
         two_l = load_list("two_l", two)
         for q in range(QUADS):
             load_scale_rows(nc.sync, w2s_raw, w2_scales, q, W2_ROW)
         xw = load_words("xw", x_words)
-        offs_l = load_list("offs_l", offs)
         for q in range(QUADS):
             load_scale_rows(nc.sync, xs, x_scales, q, 0)
-        n2_l = load_list("n2_l", n2)
+        offs_l = load_list("offs_l", offs)
         w1w_raw = load_words("w1w_raw", w1_words)
         cand_l = load_list("cand_l", cand)
-        for q in range(QUADS):
-            load_scale_rows(nc.sync, w1s_raw, w1_scales, q, W1_ROW)
+        n2_l = load_list("n2_l", n2)
         n1_l = load_list("n1_l", n1)
         n3_l = load_list("n3_l", n3)
         gain = tile("gain", [P, PACK], F32)
@@ -101,34 +111,7 @@ def tile_picked_twcclampbfrac_none_po_kernel(
             m = slice(P * t, P * (t + 1))
             nc.tensor.matmul_mx(out, lhsT=lw[:, m].bitcast(FP8X4), lhsT_scale=ls[first:P, m], rhs=rw.bitcast(FP8X4), rhs_scale=rs, start=True, stop=True)
 
-        w2w = deal("w2w", w2w_raw, U32, I32)
-        w2s = deal("w2s", w2s_raw, U8, U8)
-        two_w = pick("two_w", xw, two_l, U32)
-        two_s = pick("two_s", xs, two_l, U8)
-        d = []
-        for t in range(PACK):
-            bank = psum.tile([P, S], F32, name=f"d_ps{t}", tag=f"bank{t}")
-            product(bank[:], w2w, w2s, W2_ROW, t, two_w[:], two_s[:])
-            d_t = tile(f"d{t}", [P, S], F32)
-            nc.scalar.activation(d_t[:], bank[:], ACT.Copy)
-            d.append(d_t)
-
-        offs_w = pick("offs_w", xw, offs_l, U32)
-        offs_s = pick("offs_s", xs, offs_l, U8)
-        w1w = deal("w1w", w1w_raw, U32, I32)
-        w1s = deal("w1s", w1s_raw, U8, U8)
-        y_ps = [psum.tile([P, 2, S], F32, name=f"y_ps{u}", tag=f"bank{4 + u}") for u in range(2)]
-        for t in range(PACK):
-            product(y_ps[t // 2][:, t % 2, :], w1w, w1s, W1_ROW, t, offs_w[:], offs_s[:])
-
-        cand_w = deal("cand_w", pick("cand_w_raw", xw, cand_l, U32), U32, I32)
-        cand_s = deal("cand_s", pick("cand_s_raw", xs, cand_l, U8), U8, U8)
-
-        g1 = [tile(f"g1_{h}", [P, PACK, HALF], F32) for h in range(2)]
-        g2 = [tile(f"g2_{h}", [P, PACK, HALF], F32) for h in range(2)]
-        g3 = [tile(f"g3_{h}", [P, PACK, HALF], F32) for h in range(2)]
-        y = [tile(f"y{t}", [P, S], F32) for t in range(PACK)]
-        s = [tile(f"s{t}", [P, S], F32) for t in range(PACK)]
+        pairs = [slice(0, 2), slice(2, 4)]
 
         def blocked_rows(ap):
             return ap.rearrange("p t (c i) -> p c t i", i=4)
@@ -136,76 +119,110 @@ def tile_picked_twcclampbfrac_none_po_kernel(
         def blocked_words(ap):
             return ap.rearrange("p (c i t) -> p c t i", i=4, t=PACK)
 
-        for t in range(PACK):
-            fetch(g2[0][:, t, :], d[t], n2_l, 0)
-        for t in range(PACK):
-            nc.scalar.activation(y[t][:], y_ps[t // 2][:, t % 2, :], ACT.Copy)
+        def flat(ap):
+            return ap.rearrange("p t j -> p (t j)")
 
+        y = [window_tile(f"y{t}", S + 8) for t in range(PACK)]
+        d = [window_tile(f"d{t}", S + 8) for t in range(PACK)]
+        s = [window_tile(f"s{t}", 2 * S) for t in range(PACK)]
+        two_w = pick("two_w", xw, two_l, U32)
+        two_s = pick("two_s", xs, two_l, U8)
+        w2w = deal("w2w", w2w_raw, U32, I32)
+        w2s = deal("w2s", w2s_raw, U8, U8)
+        d_ps = [psum.tile([P, S], F32, name=f"d_ps{t}", tag=f"bank{t}") for t in range(PACK)]
+        for t in range(PACK):
+            product(d_ps[t][:], w2w, w2s, W2_ROW, t, two_w[:], two_s[:])
+        for t in range(0, 4):
+            nc.scalar.activation(d[t][:, 0:S], d_ps[t][:], ACT.Copy)
+        offs_w = pick("offs_w", xw, offs_l, U32)
+        offs_s = pick("offs_s", xs, offs_l, U8)
+        w1w = deal("w1w", w1w_raw, U32, I32)
+        w1s = deal("w1s", w1s_raw, U8, U8)
+        y_ps = [psum.tile([P, 2, S], F32, name=f"y_ps{u}", tag=f"bank{4 + u}") for u in range(2)]
+        for t in range(PACK):
+            product(y_ps[t // 2][:, t % 2, :], w1w, w1s, W1_ROW, t, offs_w[:], offs_s[:])
+        for t in range(2, 4):
+            nc.vector.tensor_copy(y[t][:, 0:S], y_ps[t // 2][:, t % 2, :])
+
+        cand_w = deal("cand_w", pick("cand_w_raw", xw, cand_l, U32, tag="w1s_raw"), U32, I32)
+        cand_s = deal("cand_s", pick("cand_s_raw", xs, cand_l, U8), U8, U8)
+
+        g1 = tile("g1", [P, PACK, S], F32)
+        g2 = tile("g2", [P, PACK, S], F32)
+        less = tile("less", [P, PACK, S], F32)
+        low = tile("low", [P, PACK, S], F32)
+        for t in range(PACK):
+            fetch(g2[:, t, :], d[t], n2_l[:])
+        for t in range(0, 2):
+            nc.scalar.activation(y[t][:, 0:S], y_ps[t // 2][:, t % 2, :], ACT.Copy)
+        for t in range(PACK):
+            fetch(g1[:, t, :], y[t], n1_l[:])
+        for u in range(2):
+            nc.vector.scalar_tensor_tensor(flat(less[:, pairs[u], :]), flat(g1[:, pairs[u], :]), -0.5, flat(y_ps[u][:]), ALU.mult, ALU.add)
         for h in range(2):
-            less = tile(f"less{h}", [P, PACK, HALF], F32)
-            low = tile(f"low{h}", [P, PACK, HALF], F32)
+            nc.vector.tensor_tensor(low[:, :, cols(h)], less[:, :, cols(h)], g2[:, :, cols(h)], ALU.min)
+        g3 = tile("g3", [P, 2, PACK, HALF], F32, tag="w1w")
+        gain_b = gain[:].unsqueeze(1).unsqueeze(3).to_broadcast([P, HALF // 4, PACK, 4])
+        s_ps = []
+        for h in range(2):
             top = tile(f"top{h}", [P, PACK, HALF], F32)
             for t in range(PACK):
-                fetch(g1[h][:, t, :], y[t], n1_l, h)
-                nc.vector.scalar_tensor_tensor(less[:, t, :], g1[h][:, t, :], -0.5, y[t][:, cols(h)], ALU.mult, ALU.add)
-            if h == 1:
-                for t in range(PACK):
-                    fetch(g2[h][:, t, :], d[t], n2_l, h)
-            for u in range(2):
-                tt = slice(2 * u, 2 * u + 2)
-                nc.vector.tensor_tensor(low[:, tt, :], less[:, tt, :], g2[h][:, tt, :], ALU.min)
-            for t in range(PACK):
-                fetch(g3[h][:, t, :], d[t], n3_l, h)
-            for u in range(2):
-                tt = slice(2 * u, 2 * u + 2)
-                nc.vector.tensor_tensor(top[:, tt, :], low[:, tt, :], g3[h][:, tt, :], ALU.max)
-            z = tile(f"z{h}", [P, PACK * HALF], BF16)
-            gain_b = gain[:].unsqueeze(1).unsqueeze(3).to_broadcast([P, HALF // 4, PACK, 4])
+                fetch(g3[:, h, t, :], d[t], entries(n3_l, h))
+            for part in ([slice(0, PACK)] if h == 0 else pairs):
+                nc.vector.tensor_tensor(top[:, part, :], low[:, part, cols(h)], g3[:, h, part, :], ALU.max)
+            z = tile(f"z{h}", [P, PACK * HALF], BF16, tag="z")
             nc.vector.tensor_tensor(blocked_words(z[:]), blocked_rows(top[:]), gain_b, ALU.mult)
             zw = tile(f"zw{h}", [P, HALF], U32)
             zs = tile(f"zs{h}", [P, HALF], U8)
             nc.vector.quantize_mx(out=zw[:].bitcast(FP8X4), scales=zs[:], in_=z[:])
+            banks = [psum.tile([P, HALF], F32, name=f"s_ps{h}_{t}", tag=f"bank{(4 + 4 * h + t) % 8}") for t in range(PACK)]
+            s_ps.append(banks)
             for t in range(PACK):
-                bank = psum.tile([P, HALF], F32, name=f"s_ps{h}_{t}", tag=f"bank{(4 + 4 * h + t) % 8}")
-                product(bank[:], cand_w, cand_s, 0, t, zw[:], zs[:])
-                if h == 1 and t % 2 == 1:
-                    nc.vector.tensor_scalar(s[t][:, cols(h)], bank[:], 0.0625, None, ALU.mult)
-                else:
-                    nc.scalar.activation(s[t][:, cols(h)], bank[:], ACT.Copy, scale=0.0625)
+                product(banks[t][:], cand_w, cand_s, 0, t, zw[:], zs[:])
 
-        g4 = [tile(f"g4_{h}", [P, PACK, HALF], F32) for h in range(2)]
-        g5 = [tile(f"g5_{h}", [P, PACK, HALF], F32) for h in range(2)]
-        size = []
         for h in range(2):
-            diff = tile(f"diff{h}", [P, PACK, HALF], F32)
-            size_h = tile(f"size{h}", [P, PACK * HALF], F32)
             for t in range(PACK):
-                fetch(g5[h][:, t, :], s[t], n5_l, h)
-                nc.vector.tensor_tensor(diff[:, t, :], g5[h][:, t, :], s[t][:, cols(h)], ALU.subtract)
-            flat = diff[:].rearrange("p t j -> p (t j)")
-            nc.vector.scalar_tensor_tensor(size_h[:], flat, -1.0, flat, ALU.mult, ALU.max)
-            size.append(size_h)
+                if h == 1 and t >= 1:
+                    nc.vector.tensor_scalar(s[t][:, cols(h)], s_ps[h][t][:], 0.0625, None, ALU.mult)
+                else:
+                    nc.scalar.activation(s[t][:, cols(h)], s_ps[h][t][:], ACT.Copy, scale=0.0625)
+
+        g5 = tile("g5", [P, PACK, S], F32)
+        diff = [tile(f"diff{u}", [P, 2, S], F32) for u in range(2)]
+        size = [tile(f"size{u}", [P, 2, S], F32) for u in range(2)]
+        for u in range(2):
+            for t in range(2 * u, 2 * u + 2):
+                fetch(g5[:, t, :], s[t], n5_l[:])
+                nc.vector.tensor_tensor(diff[u][:, t % 2, :], g5[:, t, :], s[t][:, 0:S], ALU.subtract)
+            part = flat(diff[u][:])
+            nc.vector.scalar_tensor_tensor(flat(size[u][:]), part, -1.0, part, ALU.mult, ALU.max)
 
         out_rows = out_0.rearrange("(p t) j -> p t j", t=PACK)
-        for h in range(2):
-            root = tile(f"root{h}", [P, PACK * HALF], F32)
-            inv = tile(f"inv{h}", [P, PACK * HALF], F32)
-            num = tile(f"num{h}", [P, PACK, HALF], F32)
-            res = tile(f"res{h}", [P, PACK, HALF], F32)
-            nc.scalar.activation(root[:], size[h][:], ACT.Abs_reciprocal_sqrt, bias=half_col[:])
+        res = tile("res", [P, PACK, S], F32)
+        num = tile("num", [P, PACK, S], F32)
+        for u in range(2):
+            root = tile(f"root{u}", [P, 2, S], F32)
+            inv = tile(f"inv{u}", [P, 2, S], F32)
+            nc.scalar.activation(root[:], size[u][:], ACT.Abs_reciprocal_sqrt, bias=half_col[:])
             nc.vector.tensor_tensor(inv[:], root[:], root[:], ALU.mult)
-            for t in range(PACK):
-                fetch(g4[h][:, t, :], s[t], n4_l, h)
-                nc.vector.tensor_tensor(num[:, t, :], s[t][:, cols(h)], g4[h][:, t, :], ALU.subtract)
-            nc.vector.tensor_tensor(res[:].rearrange("p t j -> p (t j)"), num[:].rearrange("p t j -> p (t j)"), inv[:], ALU.mult)
-            nc.sync.dma_start(out_rows[:, :, cols(h)], res[:])
-            rounded = tile(f"rounded{h}", [P, PACK * HALF], BF16)
-            nc.vector.tensor_copy(blocked_words(rounded[:]), blocked_rows(res[:]))
-            ow = tile(f"ow{h}", [P, HALF], U32)
-            osc = tile(f"osc{h}", [P, HALF], U8)
-            nc.vector.quantize_mx(out=ow[:].bitcast(FP8X4), scales=osc[:], in_=rounded[:])
-            words_out = out_1[0].rearrange("p n t -> p (n t)").bitcast(I32)
-            nc.sync.dma_start(words_out[:, cols(h)], ow[:].bitcast(I32))
-            for q in range(QUADS):
-                queue = nc.scalar if q % 2 == 0 else nc.sync
-                queue.dma_start(out_2[0, 4 * q : 4 * q + 4, cols(h)].bitcast(I32), osc[32 * q : 32 * q + 4, :].bitcast(I32))
+            g4 = tile(f"g4_{u}", [P, 2, S], F32, tag=f"diff{u}")
+            for t in range(2 * u, 2 * u + 2):
+                fetch(g4[:, t % 2, :], s[t], n4_l[:])
+                nc.vector.tensor_tensor(num[:, t, :], s[t][:, 0:S], g4[:, t % 2, :], ALU.subtract)
+                if u == 1:
+                    nc.vector.tensor_tensor(res[:, t, :], num[:, t, :], inv[:, t % 2, :], ALU.mult)
+            if u == 0:
+                nc.vector.tensor_tensor(res[:, pairs[u], :], num[:, pairs[u], :], inv[:], ALU.mult)
+            nc.sync.dma_start(out_rows[:, pairs[u], :], res[:, pairs[u], :])
+
+        ow = tile("ow", [P, S], U32)
+        osc = tile("osc", [P, S], U8)
+        rounded = [tile(f"rounded{h}", [P, PACK * HALF], BF16) for h in range(2)]
+        nc.vector.tensor_copy(blocked_words(rounded[0][:]), blocked_rows(res[:, :, cols(0)]))
+        nc.vector.tensor_copy(blocked_words(rounded[1][:]), blocked_rows(res[:, :, cols(1)]))
+        for h in range(2):
+            nc.vector.quantize_mx(out=ow[:, cols(h)].bitcast(FP8X4), scales=osc[:, cols(h)], in_=rounded[h][:])
+        nc.scalar.dma_start(out_1[0].rearrange("p n t -> p (n t)").bitcast(I32), ow[:].bitcast(I32))
+        for q in range(QUADS):
+            queue = nc.scalar if q % 2 == 1 else nc.sync
+            queue.dma_start(out_2[0, 4 * q : 4 * q + 4, :].bitcast(I32), osc[32 * q : 32 * q + 4, :].bitcast(I32))

@@ -17,8 +17,13 @@ ACT = mybir.ActivationFunctionType
 
 P = 128
 PACK = 4
-HALF = S // 2
 QUADS = 4
+HALF = S // 2
+PAIRS = [slice(0, 2), slice(2, 4)]
+BANKS = 8
+X_FIRST, W2_FIRST, W1_FIRST = 0, 4, 8
+WINDOW_ONE, WINDOW_EIGHT = S + 8, 2 * S
+Y_ON_SCALAR = 2
 
 
 def tile_picked_twcclampbfrac_none_po_kernel(
@@ -29,8 +34,8 @@ def tile_picked_twcclampbfrac_none_po_kernel(
         sb = ctx.enter_context(tc.tile_pool(name="sb", bufs=1))
         psum = ctx.enter_context(tc.psum_pool(name="psum", bufs=1))
 
-        def tile(name, shape, dtype, tag=None):
-            return sb.tile(shape, dtype, name=name, tag=tag or name, align_bytes=64)
+        def tile(name, shape, dtype, reuse=None):
+            return sb.tile(shape, dtype, name=name, tag=reuse or name, align_bytes=64)
 
         def load_list(name, src):
             dst = tile(name, [P, src.shape[1]], U16)
@@ -42,13 +47,15 @@ def tile_picked_twcclampbfrac_none_po_kernel(
             nc.sync.dma_start(dst[:].bitcast(I32), src[0].rearrange("p n t -> p (n t)").bitcast(I32))
             return dst
 
-        def zeroed_plane(name, width):
+        def zeroed_plane(engine, name, width):
             dst = tile(name, [P, width], U8)
-            nc.vector.memset(dst[:].bitcast(I32), 0)
+            engine.memset(dst[:].bitcast(I32), 0)
             return dst
 
-        def load_scale_rows(queue, dst, src, q, first):
-            queue.dma_start(dst[32 * q + first : 32 * q + first + 4, :].bitcast(I32), src[0, 4 * q : 4 * q + 4, :].bitcast(I32))
+        def load_scale_rows(queue, dst, src, first, quads):
+            for q in quads:
+                rows = dst[32 * q + first : 32 * q + first + 4, :]
+                queue.dma_start(rows.bitcast(I32), src[0, 4 * q : 4 * q + 4, :].bitcast(I32))
 
         def deal(name, src, dtype, view):
             dst = tile(name, [P, PACK * P], dtype)
@@ -58,171 +65,176 @@ def tile_picked_twcclampbfrac_none_po_kernel(
             )
             return dst
 
-        def pick(name, table, offsets, dtype, tag=None):
-            dst = tile(name, [P, 16 * offsets.shape[1]], dtype, tag=tag)
+        def pick(name, table, offsets, dtype):
+            dst = tile(name, [P, 16 * offsets.shape[1]], dtype)
             nc.vector.tensor_copy(dst[:], table[:].indirect(offsets[:]))
             return dst
 
         def fetch(dst, window, offsets):
             nc.scalar.activation(dst, window[:].indirect(offsets), ACT.Copy)
 
-        def entries(offsets, h):
-            return offsets[:, 8 * h : 8 * h + 8]
-
         def window_tile(name, width):
             dst = tile(name, [P, width], F32)
             nc.vector.memset(dst[:, S:width], 0.0)
             return dst
 
+        def product(out, words, plane, first, t, moving_words, moving_plane):
+            m = slice(P * t, P * (t + 1))
+            nc.tensor.matmul_mx(
+                out,
+                lhsT=words[:, m].bitcast(FP8X4),
+                lhsT_scale=plane[first:P, m],
+                rhs=moving_words.bitcast(FP8X4),
+                rhs_scale=moving_plane,
+                start=True,
+                stop=True,
+            )
+
         def cols(h):
             return slice(HALF * h, HALF * (h + 1))
-
-        W2_ROW, W1_ROW = 4, 8
-
-        w2s_raw = zeroed_plane("w2s_raw", H)
-        xs = zeroed_plane("xs", T)
-        w1s_raw = tile("w1s_raw", [P, H], U8)
-        nc.gpsimd.memset(w1s_raw[:].bitcast(I32), 0)
-        for q in range(QUADS):
-            load_scale_rows(nc.gpsimd, w1s_raw, w1_scales, q, W1_ROW)
-        half_col = tile("half_col", [P, 1], F32)
-        nc.vector.memset(half_col[:], 0.5)
-        warm = tile("warm", [P, 1], F32)
-        nc.scalar.activation(warm[:], half_col[:], ACT.Abs_reciprocal_sqrt, bias=half_col[:])
-        w2w_raw = load_words("w2w_raw", w2_words)
-        two_l = load_list("two_l", two)
-        for q in range(QUADS):
-            load_scale_rows(nc.sync, w2s_raw, w2_scales, q, W2_ROW)
-        xw = load_words("xw", x_words)
-        for q in range(QUADS):
-            load_scale_rows(nc.sync, xs, x_scales, q, 0)
-        offs_l = load_list("offs_l", offs)
-        w1w_raw = load_words("w1w_raw", w1_words)
-        cand_l = load_list("cand_l", cand)
-        n2_l = load_list("n2_l", n2)
-        n1_l = load_list("n1_l", n1)
-        n3_l = load_list("n3_l", n3)
-        gain = tile("gain", [P, PACK], F32)
-        nc.sync.dma_start(gain[:], gs.rearrange("(p t) o -> p (t o)", t=PACK))
-        n5_l = load_list("n5_l", n5)
-        n4_l = load_list("n4_l", n4)
-
-        def product(out, lw, ls, first, t, rw, rs):
-            m = slice(P * t, P * (t + 1))
-            nc.tensor.matmul_mx(out, lhsT=lw[:, m].bitcast(FP8X4), lhsT_scale=ls[first:P, m], rhs=rw.bitcast(FP8X4), rhs_scale=rs, start=True, stop=True)
-
-        pairs = [slice(0, 2), slice(2, 4)]
-
-        def blocked_rows(ap):
-            return ap.rearrange("p t (c i) -> p c t i", i=4)
-
-        def blocked_words(ap):
-            return ap.rearrange("p (c i t) -> p c t i", i=4, t=PACK)
 
         def flat(ap):
             return ap.rearrange("p t j -> p (t j)")
 
-        y = [window_tile(f"y{t}", S + 8) for t in range(PACK)]
-        d = [window_tile(f"d{t}", S + 8) for t in range(PACK)]
-        s = [window_tile(f"s{t}", 2 * S) for t in range(PACK)]
-        two_w = pick("two_w", xw, two_l, U32)
-        two_s = pick("two_s", xs, two_l, U8)
-        w2w = deal("w2w", w2w_raw, U32, I32)
-        w2s = deal("w2s", w2s_raw, U8, U8)
-        d_ps = [psum.tile([P, S], F32, name=f"d_ps{t}", tag=f"bank{t}") for t in range(PACK)]
-        for t in range(PACK):
-            product(d_ps[t][:], w2w, w2s, W2_ROW, t, two_w[:], two_s[:])
-        for t in range(0, 4):
-            nc.scalar.activation(d[t][:, 0:S], d_ps[t][:], ACT.Copy)
-        offs_w = pick("offs_w", xw, offs_l, U32)
-        offs_s = pick("offs_s", xs, offs_l, U8)
-        w1w = deal("w1w", w1w_raw, U32, I32)
-        w1s = deal("w1s", w1s_raw, U8, U8)
-        y_ps = [psum.tile([P, 2, S], F32, name=f"y_ps{u}", tag=f"bank{4 + u}") for u in range(2)]
-        for t in range(PACK):
-            product(y_ps[t // 2][:, t % 2, :], w1w, w1s, W1_ROW, t, offs_w[:], offs_s[:])
-        for t in range(2, 4):
-            nc.vector.tensor_copy(y[t][:, 0:S], y_ps[t // 2][:, t % 2, :])
+        def walk_row_tiles(ap):
+            return ap.rearrange("p t (c i) -> p c t i", i=4)
 
-        cand_w = deal("cand_w", pick("cand_w_raw", xw, cand_l, U32, tag="w1s_raw"), U32, I32)
-        cand_s = deal("cand_s", pick("cand_s_raw", xs, cand_l, U8), U8, U8)
+        def walk_interleaved(ap):
+            return ap.rearrange("p (c i t) -> p c t i", i=4, t=PACK)
 
-        g1 = tile("g1", [P, PACK, S], F32)
-        g2 = tile("g2", [P, PACK, S], F32)
+        w2_plane_in = zeroed_plane(nc.gpsimd, "w2_plane_in", H)
+        load_scale_rows(nc.gpsimd, w2_plane_in, w2_scales, W2_FIRST, range(2, QUADS))
+        x_plane = zeroed_plane(nc.vector, "x_plane", T)
+        w1_plane_in = zeroed_plane(nc.vector, "w1_plane_in", H)
+        one_half = tile("one_half", [P, 1], F32)
+        nc.vector.memset(one_half[:], 0.5)
+        warm_up = tile("warm_up", [P, 1], F32)
+        nc.scalar.activation(warm_up[:], one_half[:], ACT.Abs_reciprocal_sqrt, bias=one_half[:])
+
+        w2_words_in = load_words("w2_words_in", w2_words)
+        load_scale_rows(nc.sync, w2_plane_in, w2_scales, W2_FIRST, range(2))
+        load_scale_rows(nc.sync, x_plane, x_scales, X_FIRST, range(QUADS))
+        x_table = load_words("x_table", x_words)
+        two_list = load_list("two_list", two)
+        offs_list = load_list("offs_list", offs)
+        load_scale_rows(nc.sync, w1_plane_in, w1_scales, W1_FIRST, range(QUADS))
+        w1_words_in = load_words("w1_words_in", w1_words)
+        n2_list = load_list("n2_list", n2)
+        cand_list = load_list("cand_list", cand)
+        n1_list = load_list("n1_list", n1)
+        n3_list = load_list("n3_list", n3)
+        gain = tile("gain", [P, PACK], F32)
+        nc.sync.dma_start(gain[:], gs.rearrange("(p t) o -> p (t o)", t=PACK))
+        n5_list = load_list("n5_list", n5)
+        n4_list = load_list("n4_list", n4)
+
+        y = [window_tile(f"y{t}", WINDOW_ONE) for t in range(PACK)]
+        d = [window_tile(f"d{t}", WINDOW_ONE) for t in range(PACK)]
+        s = [window_tile(f"s{t}", WINDOW_EIGHT) for t in range(PACK)]
+
+        two_words = pick("two_words", x_table, two_list, U32)
+        two_plane = pick("two_plane", x_plane, two_list, U8)
+        w2_dealt = deal("w2_dealt", w2_words_in, U32, I32)
+        w2_plane = deal("w2_plane", w2_plane_in, U8, U8)
+        d_psum = [psum.tile([P, S], F32, name=f"d_psum{t}", tag=f"bank{t}") for t in range(PACK)]
+        for t in range(PACK):
+            product(d_psum[t][:], w2_dealt, w2_plane, W2_FIRST, t, two_words[:], two_plane[:])
+        for t in range(PACK):
+            nc.scalar.activation(d[t][:, 0:S], d_psum[t][:], ACT.Copy)
+
+        offs_words = pick("offs_words", x_table, offs_list, U32)
+        offs_plane = pick("offs_plane", x_plane, offs_list, U8)
+        w1_dealt = deal("w1_dealt", w1_words_in, U32, I32)
+        w1_plane = deal("w1_plane", w1_plane_in, U8, U8)
+        y_psum = [psum.tile([P, 2, S], F32, name=f"y_psum{u}", tag=f"bank{PACK + u}") for u in range(2)]
+        for t in range(PACK):
+            product(y_psum[t // 2][:, t % 2, :], w1_dealt, w1_plane, W1_FIRST, t, offs_words[:], offs_plane[:])
+        for t in range(Y_ON_SCALAR, PACK):
+            nc.vector.tensor_copy(y[t][:, 0:S], y_psum[t // 2][:, t % 2, :])
+
+        cand_words = deal("cand_words", pick("cand_words_picked", x_table, cand_list, U32), U32, I32)
+        cand_plane = deal("cand_plane", pick("cand_plane_picked", x_plane, cand_list, U8), U8, U8)
+
+        y_n1 = tile("y_n1", [P, PACK, S], F32)
+        d_n2 = tile("d_n2", [P, PACK, S], F32)
         less = tile("less", [P, PACK, S], F32)
         low = tile("low", [P, PACK, S], F32)
         for t in range(PACK):
-            fetch(g2[:, t, :], d[t], n2_l[:])
-        for t in range(0, 2):
-            nc.scalar.activation(y[t][:, 0:S], y_ps[t // 2][:, t % 2, :], ACT.Copy)
+            fetch(d_n2[:, t, :], d[t], n2_list[:])
+        for t in range(Y_ON_SCALAR):
+            nc.scalar.activation(y[t][:, 0:S], y_psum[t // 2][:, t % 2, :], ACT.Copy)
         for t in range(PACK):
-            fetch(g1[:, t, :], y[t], n1_l[:])
+            fetch(y_n1[:, t, :], y[t], n1_list[:])
         for u in range(2):
-            nc.vector.scalar_tensor_tensor(flat(less[:, pairs[u], :]), flat(g1[:, pairs[u], :]), -0.5, flat(y_ps[u][:]), ALU.mult, ALU.add)
+            nc.vector.scalar_tensor_tensor(
+                flat(less[:, PAIRS[u], :]), flat(y_n1[:, PAIRS[u], :]), -0.5, flat(y_psum[u][:]), ALU.mult, ALU.add
+            )
         for h in range(2):
-            nc.vector.tensor_tensor(low[:, :, cols(h)], less[:, :, cols(h)], g2[:, :, cols(h)], ALU.min)
-        g3 = tile("g3", [P, 2, PACK, HALF], F32, tag="w1w")
-        gain_b = gain[:].unsqueeze(1).unsqueeze(3).to_broadcast([P, HALF // 4, PACK, 4])
-        s_ps = []
+            nc.vector.tensor_tensor(low[:, :, cols(h)], less[:, :, cols(h)], d_n2[:, :, cols(h)], ALU.min)
+
+        d_n3 = tile("d_n3", [P, 2, PACK, HALF], F32, reuse="w1_dealt")
+        gain_walk = gain[:].unsqueeze(1).unsqueeze(3).to_broadcast([P, HALF // 4, PACK, 4])
+        s_psum = []
         for h in range(2):
             top = tile(f"top{h}", [P, PACK, HALF], F32)
             for t in range(PACK):
-                fetch(g3[:, h, t, :], d[t], entries(n3_l, h))
-            for part in ([slice(0, PACK)] if h == 0 else pairs):
-                nc.vector.tensor_tensor(top[:, part, :], low[:, part, cols(h)], g3[:, h, part, :], ALU.max)
-            z = tile(f"z{h}", [P, PACK * HALF], BF16, tag="z")
-            nc.vector.tensor_tensor(blocked_words(z[:]), blocked_rows(top[:]), gain_b, ALU.mult)
-            zw = tile(f"zw{h}", [P, HALF], U32)
-            zs = tile(f"zs{h}", [P, HALF], U8)
-            nc.vector.quantize_mx(out=zw[:].bitcast(FP8X4), scales=zs[:], in_=z[:])
-            banks = [psum.tile([P, HALF], F32, name=f"s_ps{h}_{t}", tag=f"bank{(4 + 4 * h + t) % 8}") for t in range(PACK)]
-            s_ps.append(banks)
+                fetch(d_n3[:, h, t, :], d[t], n3_list[:, HALF // 16 * h : HALF // 16 * (h + 1)])
+            for part in [slice(0, PACK)] if h == 0 else PAIRS:
+                nc.vector.tensor_tensor(top[:, part, :], low[:, part, cols(h)], d_n3[:, h, part, :], ALU.max)
+            z = tile(f"z{h}", [P, PACK * HALF], BF16, reuse="z")
+            nc.vector.tensor_tensor(walk_interleaved(z[:]), walk_row_tiles(top[:]), gain_walk, ALU.mult)
+            z_words = tile(f"z_words{h}", [P, HALF], U32)
+            z_plane = tile(f"z_plane{h}", [P, HALF], U8)
+            nc.vector.quantize_mx(out=z_words[:].bitcast(FP8X4), scales=z_plane[:], in_=z[:])
+            banks = [
+                psum.tile([P, HALF], F32, name=f"s_psum{h}_{t}", tag=f"bank{(PACK * (h + 1) + t) % BANKS}") for t in range(PACK)
+            ]
+            s_psum.append(banks)
             for t in range(PACK):
-                product(banks[t][:], cand_w, cand_s, 0, t, zw[:], zs[:])
+                product(banks[t][:], cand_words, cand_plane, X_FIRST, t, z_words[:], z_plane[:])
 
         for h in range(2):
             for t in range(PACK):
-                if h == 1 and t >= 1:
-                    nc.vector.tensor_scalar(s[t][:, cols(h)], s_ps[h][t][:], 0.0625, None, ALU.mult)
+                if h == 1 and t > 0:
+                    nc.vector.tensor_scalar(s[t][:, cols(h)], s_psum[h][t][:], 0.0625, None, ALU.mult)
                 else:
-                    nc.scalar.activation(s[t][:, cols(h)], s_ps[h][t][:], ACT.Copy, scale=0.0625)
+                    nc.scalar.activation(s[t][:, cols(h)], s_psum[h][t][:], ACT.Copy, scale=0.0625)
 
-        g5 = tile("g5", [P, PACK, S], F32)
+        s_n5 = tile("s_n5", [P, PACK, S], F32)
         diff = [tile(f"diff{u}", [P, 2, S], F32) for u in range(2)]
         size = [tile(f"size{u}", [P, 2, S], F32) for u in range(2)]
         for u in range(2):
             for t in range(2 * u, 2 * u + 2):
-                fetch(g5[:, t, :], s[t], n5_l[:])
-                nc.vector.tensor_tensor(diff[u][:, t % 2, :], g5[:, t, :], s[t][:, 0:S], ALU.subtract)
-            part = flat(diff[u][:])
-            nc.vector.scalar_tensor_tensor(flat(size[u][:]), part, -1.0, part, ALU.mult, ALU.max)
+                fetch(s_n5[:, t, :], s[t], n5_list[:])
+                nc.vector.tensor_tensor(diff[u][:, t % 2, :], s_n5[:, t, :], s[t][:, 0:S], ALU.subtract)
+            nc.vector.scalar_tensor_tensor(flat(size[u][:]), flat(diff[u][:]), -1.0, flat(diff[u][:]), ALU.mult, ALU.max)
 
         out_rows = out_0.rearrange("(p t) j -> p t j", t=PACK)
-        res = tile("res", [P, PACK, S], F32)
-        num = tile("num", [P, PACK, S], F32)
+        result = tile("result", [P, PACK, S], F32)
+        numerator = tile("numerator", [P, PACK, S], F32)
         for u in range(2):
             root = tile(f"root{u}", [P, 2, S], F32)
-            inv = tile(f"inv{u}", [P, 2, S], F32)
-            nc.scalar.activation(root[:], size[u][:], ACT.Abs_reciprocal_sqrt, bias=half_col[:])
-            nc.vector.tensor_tensor(inv[:], root[:], root[:], ALU.mult)
-            g4 = tile(f"g4_{u}", [P, 2, S], F32, tag=f"diff{u}")
-            for t in range(2 * u, 2 * u + 2):
-                fetch(g4[:, t % 2, :], s[t], n4_l[:])
-                nc.vector.tensor_tensor(num[:, t, :], s[t][:, 0:S], g4[:, t % 2, :], ALU.subtract)
-                if u == 1:
-                    nc.vector.tensor_tensor(res[:, t, :], num[:, t, :], inv[:, t % 2, :], ALU.mult)
+            inverse = tile(f"inverse{u}", [P, 2, S], F32)
+            nc.scalar.activation(root[:], size[u][:], ACT.Abs_reciprocal_sqrt, bias=one_half[:])
             if u == 0:
-                nc.vector.tensor_tensor(res[:, pairs[u], :], num[:, pairs[u], :], inv[:], ALU.mult)
-            nc.sync.dma_start(out_rows[:, pairs[u], :], res[:, pairs[u], :])
+                nc.vector.tensor_tensor(inverse[:], root[:], root[:], ALU.mult)
+            else:
+                nc.scalar.activation(inverse[:], root[:], ACT.Square)
+            for t in range(2 * u, 2 * u + 2):
+                s_n4 = tile(f"s_n4_{t}", [P, S], F32, reuse=f"diff{u}" if t % 2 == 0 else None)
+                fetch(s_n4[:], s[t], n4_list[:])
+                nc.vector.tensor_tensor(numerator[:, t, :], s[t][:, 0:S], s_n4[:], ALU.subtract)
+            nc.vector.tensor_tensor(result[:, PAIRS[u], :], numerator[:, PAIRS[u], :], inverse[:], ALU.mult)
+            nc.sync.dma_start(out_rows[:, PAIRS[u], :], result[:, PAIRS[u], :])
 
-        ow = tile("ow", [P, S], U32)
-        osc = tile("osc", [P, S], U8)
+        out_words = tile("out_words", [P, S], U32)
+        out_plane = tile("out_plane", [P, S], U8)
         rounded = [tile(f"rounded{h}", [P, PACK * HALF], BF16) for h in range(2)]
-        nc.vector.tensor_copy(blocked_words(rounded[0][:]), blocked_rows(res[:, :, cols(0)]))
-        nc.vector.tensor_copy(blocked_words(rounded[1][:]), blocked_rows(res[:, :, cols(1)]))
+        nc.vector.tensor_copy(walk_interleaved(rounded[0][:]), walk_row_tiles(result[:, :, cols(0)]))
+        nc.scalar.copy(walk_interleaved(rounded[1][:]), walk_row_tiles(result[:, :, cols(1)]))
         for h in range(2):
-            nc.vector.quantize_mx(out=ow[:, cols(h)].bitcast(FP8X4), scales=osc[:, cols(h)], in_=rounded[h][:])
-        nc.scalar.dma_start(out_1[0].rearrange("p n t -> p (n t)").bitcast(I32), ow[:].bitcast(I32))
+            nc.vector.quantize_mx(out=out_words[:, cols(h)].bitcast(FP8X4), scales=out_plane[:, cols(h)], in_=rounded[h][:])
+        nc.scalar.dma_start(out_1[0].rearrange("p n t -> p (n t)").bitcast(I32), out_words[:].bitcast(I32))
         for q in range(QUADS):
             queue = nc.scalar if q % 2 == 1 else nc.sync
-            queue.dma_start(out_2[0, 4 * q : 4 * q + 4, :].bitcast(I32), osc[32 * q : 32 * q + 4, :].bitcast(I32))
+            queue.dma_start(out_2[0, 4 * q : 4 * q + 4, :].bitcast(I32), out_plane[32 * q : 32 * q + 4, :].bitcast(I32))

@@ -23,7 +23,6 @@ PAIRS = [slice(0, 2), slice(2, 4)]
 BANKS = 8
 X_FIRST, W2_FIRST, W1_FIRST = 0, 4, 8
 WINDOW_ONE, WINDOW_EIGHT = S + 8, 2 * S
-Y_ON_SCALAR = 2
 
 
 def tile_picked_twcclampbfrac_none_po_kernel(
@@ -52,21 +51,21 @@ def tile_picked_twcclampbfrac_none_po_kernel(
             engine.memset(dst[:].bitcast(I32), 0)
             return dst
 
-        def load_scale_rows(queue, dst, src, first, quads):
+        def load_scale_rows(queue, dst, src, first, quads=range(QUADS)):
             for q in quads:
                 rows = dst[32 * q + first : 32 * q + first + 4, :]
                 queue.dma_start(rows.bitcast(I32), src[0, 4 * q : 4 * q + 4, :].bitcast(I32))
 
-        def deal(name, src, dtype, view):
-            dst = tile(name, [P, PACK * P], dtype)
+        def deal(name, src, dtype, view, reuse=None):
+            dst = tile(name, [P, PACK * P], dtype, reuse)
             nc.vector.tensor_copy(
                 dst[:].bitcast(view).rearrange("p (t m) -> p m t", t=PACK),
                 src[:].bitcast(view).rearrange("p (m t) -> p m t", t=PACK),
             )
             return dst
 
-        def pick(name, table, offsets, dtype):
-            dst = tile(name, [P, 16 * offsets.shape[1]], dtype)
+        def pick(name, table, offsets, dtype, reuse=None):
+            dst = tile(name, [P, 16 * offsets.shape[1]], dtype, reuse)
             nc.vector.tensor_copy(dst[:], table[:].indirect(offsets[:]))
             return dst
 
@@ -102,86 +101,82 @@ def tile_picked_twcclampbfrac_none_po_kernel(
         def walk_interleaved(ap):
             return ap.rearrange("p (c i t) -> p c t i", i=4, t=PACK)
 
-        w2_plane_in = zeroed_plane(nc.gpsimd, "w2_plane_in", H)
-        load_scale_rows(nc.gpsimd, w2_plane_in, w2_scales, W2_FIRST, range(2, QUADS))
+        w1_plane_in = zeroed_plane(nc.gpsimd, "w1_plane_in", H)
+        load_scale_rows(nc.gpsimd, w1_plane_in, w1_scales, W1_FIRST, range(2, QUADS))
         x_plane = zeroed_plane(nc.vector, "x_plane", T)
-        w1_plane_in = zeroed_plane(nc.vector, "w1_plane_in", H)
+        w2_plane_in = zeroed_plane(nc.vector, "w2_plane_in", H)
         one_half = tile("one_half", [P, 1], F32)
         nc.vector.memset(one_half[:], 0.5)
         warm_up = tile("warm_up", [P, 1], F32)
         nc.scalar.activation(warm_up[:], one_half[:], ACT.Abs_reciprocal_sqrt, bias=one_half[:])
+        y = [window_tile(f"y{t}", WINDOW_ONE) for t in range(PACK)]
+        d = [window_tile(f"d{t}", WINDOW_ONE) for t in range(PACK)]
+        s = [window_tile(f"s{t}", WINDOW_EIGHT) for t in range(PACK)]
 
-        w2_words_in = load_words("w2_words_in", w2_words)
-        load_scale_rows(nc.sync, w2_plane_in, w2_scales, W2_FIRST, range(2))
-        load_scale_rows(nc.sync, x_plane, x_scales, X_FIRST, range(QUADS))
-        x_table = load_words("x_table", x_words)
-        two_list = load_list("two_list", two)
-        offs_list = load_list("offs_list", offs)
-        load_scale_rows(nc.sync, w1_plane_in, w1_scales, W1_FIRST, range(QUADS))
         w1_words_in = load_words("w1_words_in", w1_words)
-        n2_list = load_list("n2_list", n2)
+        load_scale_rows(nc.sync, x_plane, x_scales, X_FIRST)
+        offs_list = load_list("offs_list", offs)
         cand_list = load_list("cand_list", cand)
+        x_table = load_words("x_table", x_words)
+        load_scale_rows(nc.sync, w1_plane_in, w1_scales, W1_FIRST, range(2))
+        two_list = load_list("two_list", two)
         n1_list = load_list("n1_list", n1)
+        w2_words_in = load_words("w2_words_in", w2_words)
+        load_scale_rows(nc.sync, w2_plane_in, w2_scales, W2_FIRST)
+        n2_list = load_list("n2_list", n2)
         n3_list = load_list("n3_list", n3)
         gain = tile("gain", [P, PACK], F32)
         nc.sync.dma_start(gain[:], gs.rearrange("(p t) o -> p (t o)", t=PACK))
         n5_list = load_list("n5_list", n5)
         n4_list = load_list("n4_list", n4)
 
-        y = [window_tile(f"y{t}", WINDOW_ONE) for t in range(PACK)]
-        d = [window_tile(f"d{t}", WINDOW_ONE) for t in range(PACK)]
-        s = [window_tile(f"s{t}", WINDOW_EIGHT) for t in range(PACK)]
-
-        two_words = pick("two_words", x_table, two_list, U32)
-        two_plane = pick("two_plane", x_plane, two_list, U8)
-        w2_dealt = deal("w2_dealt", w2_words_in, U32, I32)
-        w2_plane = deal("w2_plane", w2_plane_in, U8, U8)
-        d_psum = [psum.tile([P, S], F32, name=f"d_psum{t}", tag=f"bank{t}") for t in range(PACK)]
-        for t in range(PACK):
-            product(d_psum[t][:], w2_dealt, w2_plane, W2_FIRST, t, two_words[:], two_plane[:])
-        for t in range(PACK):
-            nc.scalar.activation(d[t][:, 0:S], d_psum[t][:], ACT.Copy)
-
         offs_words = pick("offs_words", x_table, offs_list, U32)
         offs_plane = pick("offs_plane", x_plane, offs_list, U8)
         w1_dealt = deal("w1_dealt", w1_words_in, U32, I32)
         w1_plane = deal("w1_plane", w1_plane_in, U8, U8)
-        y_psum = [psum.tile([P, 2, S], F32, name=f"y_psum{u}", tag=f"bank{PACK + u}") for u in range(2)]
+        y_psum = [psum.tile([P, S], F32, name=f"y_psum{t}", tag=f"bank{PACK + t}") for t in range(PACK)]
         for t in range(PACK):
-            product(y_psum[t // 2][:, t % 2, :], w1_dealt, w1_plane, W1_FIRST, t, offs_words[:], offs_plane[:])
-        for t in range(Y_ON_SCALAR, PACK):
-            nc.vector.tensor_copy(y[t][:, 0:S], y_psum[t // 2][:, t % 2, :])
+            product(y_psum[t][:], w1_dealt, w1_plane, W1_FIRST, t, offs_words[:], offs_plane[:])
+        for t in range(PACK):
+            nc.scalar.activation(y[t][:, 0:S], y_psum[t][:], ACT.Copy)
 
-        cand_words = deal("cand_words", pick("cand_words_picked", x_table, cand_list, U32), U32, I32)
-        cand_plane = deal("cand_plane", pick("cand_plane_picked", x_plane, cand_list, U8), U8, U8)
+        two_words = pick("two_words", x_table, two_list, U32)
+        two_plane = pick("two_plane", x_plane, two_list, U8)
+        w2_dealt = deal("w2_dealt", w2_words_in, U32, I32)
+        w2_plane = deal("w2_plane", w2_plane_in, U8, U8, reuse="offs_plane")
+        d_psum = [psum.tile([P, S], F32, name=f"d_psum{t}", tag=f"bank{t}") for t in range(PACK)]
+        for t in range(PACK):
+            product(d_psum[t][:], w2_dealt, w2_plane, W2_FIRST, t, two_words[:], two_plane[:])
+        for t in range(PACK):
+            nc.vector.tensor_copy(d[t][:, 0:S], d_psum[t][:])
+
+        cand_words_picked = pick("cand_words_picked", x_table, cand_list, U32, reuse="w2_plane_in")
+        cand_words = deal("cand_words", cand_words_picked, U32, I32)
+        cand_plane_picked = pick("cand_plane_picked", x_plane, cand_list, U8)
+        cand_plane = deal("cand_plane", cand_plane_picked, U8, U8, reuse="offs_words")
 
         y_n1 = tile("y_n1", [P, PACK, S], F32)
         d_n2 = tile("d_n2", [P, PACK, S], F32)
-        less = tile("less", [P, PACK, S], F32)
+        less = tile("less", [P, PACK, S], F32, reuse="w2_plane_in")
         low = tile("low", [P, PACK, S], F32)
         for t in range(PACK):
-            fetch(d_n2[:, t, :], d[t], n2_list[:])
-        for t in range(Y_ON_SCALAR):
-            nc.scalar.activation(y[t][:, 0:S], y_psum[t // 2][:, t % 2, :], ACT.Copy)
-        for t in range(PACK):
             fetch(y_n1[:, t, :], y[t], n1_list[:])
-        for u in range(2):
-            nc.vector.scalar_tensor_tensor(
-                flat(less[:, PAIRS[u], :]), flat(y_n1[:, PAIRS[u], :]), -0.5, flat(y_psum[u][:]), ALU.mult, ALU.add
-            )
-        for h in range(2):
-            nc.vector.tensor_tensor(low[:, :, cols(h)], less[:, :, cols(h)], d_n2[:, :, cols(h)], ALU.min)
+            nc.vector.scalar_tensor_tensor(less[:, t, :], y_n1[:, t, :], -0.5, y_psum[t][:], ALU.mult, ALU.add)
+        for pair in PAIRS:
+            for t in range(pair.start, pair.stop):
+                fetch(d_n2[:, t, :], d[t], n2_list[:])
+            nc.vector.tensor_tensor(low[:, pair, :], less[:, pair, :], d_n2[:, pair, :], ALU.min)
 
-        d_n3 = tile("d_n3", [P, 2, PACK, HALF], F32, reuse="w1_dealt")
+        d_n3 = tile("d_n3", [P, 2, PACK, HALF], F32)
         gain_walk = gain[:].unsqueeze(1).unsqueeze(3).to_broadcast([P, HALF // 4, PACK, 4])
         s_psum = []
         for h in range(2):
             top = tile(f"top{h}", [P, PACK, HALF], F32)
             for t in range(PACK):
                 fetch(d_n3[:, h, t, :], d[t], n3_list[:, HALF // 16 * h : HALF // 16 * (h + 1)])
-            for part in [slice(0, PACK)] if h == 0 else PAIRS:
-                nc.vector.tensor_tensor(top[:, part, :], low[:, part, cols(h)], d_n3[:, h, part, :], ALU.max)
-            z = tile(f"z{h}", [P, PACK * HALF], BF16, reuse="z")
+            for pair in PAIRS:
+                nc.vector.tensor_tensor(top[:, pair, :], low[:, pair, cols(h)], d_n3[:, h, pair, :], ALU.max)
+            z = tile(f"z{h}", [P, PACK * HALF], BF16)
             nc.vector.tensor_tensor(walk_interleaved(z[:]), walk_row_tiles(top[:]), gain_walk, ALU.mult)
             z_words = tile(f"z_words{h}", [P, HALF], U32)
             z_plane = tile(f"z_plane{h}", [P, HALF], U8)

from contextlib import ExitStack

import concourse.mybir as mybir

K, T, S, H, C = 512, 2048, 256, 512, 512
FLOPS = 2 * K * H * S * 2 + 2 * K * C * S

F32 = mybir.dt.float32
BF16 = mybir.dt.bfloat16
I32 = mybir.dt.int32
U32 = mybir.dt.uint32
U16 = mybir.dt.uint16
U8 = mybir.dt.uint8
FP8X4 = mybir.dt.float8_e4m3fn_x4
ALU = mybir.AluOpType
ACT = mybir.ActivationFunctionType

P = 128
PACK = 4
QUADS = 4
HALF = S // 2
PAIRS = [slice(0, 2), slice(2, 4)]
BANKS = 8
X_FIRST, W2_FIRST, W1_FIRST = 0, 4, 8
WINDOW_ONE, WINDOW_EIGHT = S + 8, 2 * S


def tile_picked_twcclampbfrac_none_po_kernel(
    tc, x_words, x_scales, w1_words, w1_scales, w2_words, w2_scales, gs, offs, two, n1, n2, n3, cand, n4, n5, out_0, out_1, out_2
):
    nc = tc.nc
    with ExitStack() as ctx:
        sb = ctx.enter_context(tc.tile_pool(name="sb", bufs=1))
        psum = ctx.enter_context(tc.psum_pool(name="psum", bufs=1))

        def tile(name, shape, dtype, reuse=None):
            return sb.tile(shape, dtype, name=name, tag=reuse or name, align_bytes=64)

        def load_list(name, src):
            dst = tile(name, [P, src.shape[1]], U16)
            nc.sync.dma_start(dst[:], src)
            return dst

        def load_words(name, src):
            dst = tile(name, [P, src.shape[2]], U32)
            nc.sync.dma_start(dst[:].bitcast(I32), src[0].rearrange("p n t -> p (n t)").bitcast(I32))
            return dst

        def zeroed_plane(engine, name, width):
            dst = tile(name, [P, width], U8)
            engine.memset(dst[:].bitcast(I32), 0)
            return dst

        def load_scale_rows(queue, dst, src, first, quads=range(QUADS)):
            for q in quads:
                rows = dst[32 * q + first : 32 * q + first + 4, :]
                queue.dma_start(rows.bitcast(I32), src[0, 4 * q : 4 * q + 4, :].bitcast(I32))

        def deal(name, src, dtype, view, reuse=None):
            dst = tile(name, [P, PACK * P], dtype, reuse)
            nc.vector.tensor_copy(
                dst[:].bitcast(view).rearrange("p (t m) -> p m t", t=PACK),
                src[:].bitcast(view).rearrange("p (m t) -> p m t", t=PACK),
            )
            return dst

        def pick(name, table, offsets, dtype, reuse=None):
            dst = tile(name, [P, 16 * offsets.shape[1]], dtype, reuse)
            nc.vector.tensor_copy(dst[:], table[:].indirect(offsets[:]))
            return dst

        def fetch(dst, window, offsets):
            nc.scalar.activation(dst, window[:].indirect(offsets), ACT.Copy)

        def window_tile(name, width):
            dst = tile(name, [P, width], F32)
            nc.vector.memset(dst[:, S:width], 0.0)
            return dst

        def product(out, words, plane, first, t, moving_words, moving_plane):
            m = slice(P * t, P * (t + 1))
            nc.tensor.matmul_mx(
                out,
                lhsT=words[:, m].bitcast(FP8X4),
                lhsT_scale=plane[first:P, m],
                rhs=moving_words.bitcast(FP8X4),
                rhs_scale=moving_plane,
                start=True,
                stop=True,
            )

        def cols(h):
            return slice(HALF * h, HALF * (h + 1))

        def flat(ap):
            return ap.rearrange("p t j -> p (t j)")

        def walk_row_tiles(ap):
            return ap.rearrange("p t (c i) -> p c t i", i=4)

        def walk_interleaved(ap):
            return ap.rearrange("p (c i t) -> p c t i", i=4, t=PACK)

        w1_plane_in = zeroed_plane(nc.gpsimd, "w1_plane_in", H)
        load_scale_rows(nc.gpsimd, w1_plane_in, w1_scales, W1_FIRST, range(2, QUADS))
        x_plane = zeroed_plane(nc.vector, "x_plane", T)
        w2_plane_in = zeroed_plane(nc.vector, "w2_plane_in", H)
        one_half = tile("one_half", [P, 1], F32)
        nc.vector.memset(one_half[:], 0.5)
        warm_up = tile("warm_up", [P, 1], F32)
        nc.scalar.activation(warm_up[:], one_half[:], ACT.Abs_reciprocal_sqrt, bias=one_half[:])
        y = [window_tile(f"y{t}", WINDOW_ONE) for t in range(PACK)]
        d = [window_tile(f"d{t}", WINDOW_ONE) for t in range(PACK)]
        s = [window_tile(f"s{t}", WINDOW_EIGHT) for t in range(PACK)]

        w1_words_in = load_words("w1_words_in", w1_words)
        load_scale_rows(nc.sync, x_plane, x_scales, X_FIRST)
        offs_list = load_list("offs_list", offs)
        cand_list = load_list("cand_list", cand)
        x_table = load_words("x_table", x_words)
        load_scale_rows(nc.sync, w1_plane_in, w1_scales, W1_FIRST, range(2))
        two_list = load_list("two_list", two)
        n1_list = load_list("n1_list", n1)
        w2_words_in = load_words("w2_words_in", w2_words)
        load_scale_rows(nc.sync, w2_plane_in, w2_scales, W2_FIRST)
        n2_list = load_list("n2_list", n2)
        n3_list = load_list("n3_list", n3)
        gain = tile("gain", [P, PACK], F32)
        nc.sync.dma_start(gain[:], gs.rearrange("(p t) o -> p (t o)", t=PACK))
        n5_list = load_list("n5_list", n5)
        n4_list = load_list("n4_list", n4)

        offs_words = pick("offs_words", x_table, offs_list, U32)
        offs_plane = pick("offs_plane", x_plane, offs_list, U8)
        w1_dealt = deal("w1_dealt", w1_words_in, U32, I32)
        w1_plane = deal("w1_plane", w1_plane_in, U8, U8)
        y_psum = [psum.tile([P, S], F32, name=f"y_psum{t}", tag=f"bank{PACK + t}") for t in range(PACK)]
        for t in range(PACK):
            product(y_psum[t][:], w1_dealt, w1_plane, W1_FIRST, t, offs_words[:], offs_plane[:])
        for t in range(PACK):
            nc.scalar.activation(y[t][:, 0:S], y_psum[t][:], ACT.Copy)

        two_words = pick("two_words", x_table, two_list, U32)
        two_plane = pick("two_plane", x_plane, two_list, U8)
        w2_dealt = deal("w2_dealt", w2_words_in, U32, I32)
        w2_plane = deal("w2_plane", w2_plane_in, U8, U8, reuse="offs_plane")
        d_psum = [psum.tile([P, S], F32, name=f"d_psum{t}", tag=f"bank{t}") for t in range(PACK)]
        for t in range(PACK):
            product(d_psum[t][:], w2_dealt, w2_plane, W2_FIRST, t, two_words[:], two_plane[:])
        for t in range(PACK):
            nc.vector.tensor_copy(d[t][:, 0:S], d_psum[t][:])

        cand_words_picked = pick("cand_words_picked", x_table, cand_list, U32, reuse="w2_plane_in")
        cand_words = deal("cand_words", cand_words_picked, U32, I32)
        cand_plane_picked = pick("cand_plane_picked", x_plane, cand_list, U8)
        cand_plane = deal("cand_plane", cand_plane_picked, U8, U8, reuse="offs_words")

        y_n1 = tile("y_n1", [P, PACK, S], F32)
        d_n2 = tile("d_n2", [P, PACK, S], F32)
        less = tile("less", [P, PACK, S], F32, reuse="w2_plane_in")
        low = tile("low", [P, PACK, S], F32)
        for t in range(PACK):
            fetch(y_n1[:, t, :], y[t], n1_list[:])
            nc.vector.scalar_tensor_tensor(less[:, t, :], y_n1[:, t, :], -0.5, y_psum[t][:], ALU.mult, ALU.add)
        for pair in PAIRS:
            for t in range(pair.start, pair.stop):
                fetch(d_n2[:, t, :], d[t], n2_list[:])
            nc.vector.tensor_tensor(low[:, pair, :], less[:, pair, :], d_n2[:, pair, :], ALU.min)

        d_n3 = tile("d_n3", [P, 2, PACK, HALF], F32)
        gain_walk = gain[:].unsqueeze(1).unsqueeze(3).to_broadcast([P, HALF // 4, PACK, 4])
        s_psum = []
        for h in range(2):
            top = tile(f"top{h}", [P, PACK, HALF], F32)
            for t in range(PACK):
                fetch(d_n3[:, h, t, :], d[t], n3_list[:, HALF // 16 * h : HALF // 16 * (h + 1)])
            for pair in PAIRS:
                nc.vector.tensor_tensor(top[:, pair, :], low[:, pair, cols(h)], d_n3[:, h, pair, :], ALU.max)
            z = tile(f"z{h}", [P, PACK * HALF], BF16)
            nc.vector.tensor_tensor(walk_interleaved(z[:]), walk_row_tiles(top[:]), gain_walk, ALU.mult)
            z_words = tile(f"z_words{h}", [P, HALF], U32)
            z_plane = tile(f"z_plane{h}", [P, HALF], U8)
            nc.vector.quantize_mx(out=z_words[:].bitcast(FP8X4), scales=z_plane[:], in_=z[:])
            banks = [
                psum.tile([P, HALF], F32, name=f"s_psum{h}_{t}", tag=f"bank{(PACK * (h + 1) + t) % BANKS}") for t in range(PACK)
            ]
            s_psum.append(banks)
            for t in range(PACK):
                product(banks[t][:], cand_words, cand_plane, X_FIRST, t, z_words[:], z_plane[:])

        for h in range(2):
            for t in range(PACK):
                if h == 1 and t > 0:
                    nc.vector.tensor_scalar(s[t][:, cols(h)], s_psum[h][t][:], 0.0625, None, ALU.mult)
                else:
                    nc.scalar.activation(s[t][:, cols(h)], s_psum[h][t][:], ACT.Copy, scale=0.0625)

        s_n5 = tile("s_n5", [P, PACK, S], F32)
        diff = [tile(f"diff{u}", [P, 2, S], F32) for u in range(2)]
        size = [tile(f"size{u}", [P, 2, S], F32) for u in range(2)]
        for u in range(2):
            for t in range(2 * u, 2 * u + 2):
                fetch(s_n5[:, t, :], s[t], n5_list[:])
                nc.vector.tensor_tensor(diff[u][:, t % 2, :], s_n5[:, t, :], s[t][:, 0:S], ALU.subtract)
            nc.vector.scalar_tensor_tensor(flat(size[u][:]), flat(diff[u][:]), -1.0, flat(diff[u][:]), ALU.mult, ALU.max)

        out_rows = out_0.rearrange("(p t) j -> p t j", t=PACK)
        result = tile("result", [P, PACK, S], F32)
        numerator = tile("numerator", [P, PACK, S], F32)
        for u in range(2):
            root = tile(f"root{u}", [P, 2, S], F32)
            inverse = tile(f"inverse{u}", [P, 2, S], F32)
            nc.scalar.activation(root[:], size[u][:], ACT.Abs_reciprocal_sqrt, bias=one_half[:])
            if u == 0:
                nc.vector.tensor_tensor(inverse[:], root[:], root[:], ALU.mult)
            else:
                nc.scalar.activation(inverse[:], root[:], ACT.Square)
            for t in range(2 * u, 2 * u + 2):
                s_n4 = tile(f"s_n4_{t}", [P, S], F32, reuse=f"diff{u}" if t % 2 == 0 else None)
                fetch(s_n4[:], s[t], n4_list[:])
                nc.vector.tensor_tensor(numerator[:, t, :], s[t][:, 0:S], s_n4[:], ALU.subtract)
            nc.vector.tensor_tensor(result[:, PAIRS[u], :], numerator[:, PAIRS[u], :], inverse[:], ALU.mult)
            nc.sync.dma_start(out_rows[:, PAIRS[u], :], result[:, PAIRS[u], :])

        out_words = tile("out_words", [P, S], U32)
        out_plane = tile("out_plane", [P, S], U8)
        rounded = [tile(f"rounded{h}", [P, PACK * HALF], BF16) for h in range(2)]
        nc.vector.tensor_copy(walk_interleaved(rounded[0][:]), walk_row_tiles(result[:, :, cols(0)]))
        nc.scalar.copy(walk_interleaved(rounded[1][:]), walk_row_tiles(result[:, :, cols(1)]))
        for h in range(2):
            nc.vector.quantize_mx(out=out_words[:, cols(h)].bitcast(FP8X4), scales=out_plane[:, cols(h)], in_=rounded[h][:])
        nc.scalar.dma_start(out_1[0].rearrange("p n t -> p (n t)").bitcast(I32), out_words[:].bitcast(I32))
        for q in range(QUADS):
            queue = nc.scalar if q % 2 == 1 else nc.sync
            queue.dma_start(out_2[0, 4 * q : 4 * q + 4, :].bitcast(I32), out_plane[32 * q : 32 * q + 4, :].bitcast(I32))
